import numpy as np
import ml_dtypes


def mxq(x, axis, fmt="e4m3"):
    dtype, down = {"e4m3": (ml_dtypes.float8_e4m3fn, 7), "e5m2": (ml_dtypes.float8_e5m2, 14)}[fmt]
    v = np.moveaxis(np.asarray(x, np.float32).astype(ml_dtypes.bfloat16).astype(np.float64), axis, -1)
    blocks = v.reshape(v.shape[:-1] + (-1, 32))
    amax = np.abs(blocks).max(-1, keepdims=True)
    byte = np.maximum(np.where(amax > 0, np.frexp(amax)[1] - 1 + 127, 0) - down, 1)
    scale = np.exp2(byte - 127.0)
    codes = (blocks / scale).astype(np.float32).astype(dtype).astype(np.float64)
    return np.moveaxis((codes * scale).reshape(v.shape), -1, axis)


WIDE = False


def mx_kscale(k):
    if not WIDE:
        return np.ones(k)
    levels = np.array([10, -10, 5, -5, 0])
    if k % 512:
        return np.exp2(np.random.permutation(np.resize(levels, k // 32))).repeat(32)
    a = np.empty((k // 512, 16))
    for p in range(k // 512):
        a[p, :8] = np.random.permutation(np.resize(levels, 8))
        for g in range(8):
            far = levels[np.abs(levels - a[p, g]) >= 10]
            a[p, g + 8] = far[np.random.randint(len(far))]
    return np.exp2(a.ravel()).repeat(32)


def f64(x):
    return np.asarray(x).astype(np.float64)


def striped8(idx):
    return np.asarray(idx).reshape(8, -1, 16).transpose(0, 2, 1).reshape(128, -1).astype(np.uint16)


def unstriped8(offs):
    return offs.reshape(8, 16, -1).transpose(0, 2, 1).reshape(8, -1).astype(np.int64)


def pick8(x, idx, run):
    r = np.arange(len(x))
    return x[r[:, None], idx[r % (8 * run) // run]]


E2M1 = np.array([0.0, 0.5, 1.0, 1.5, 2.0, 3.0, 4.0, 6.0, -0.0, -0.5, -1.0, -1.5, -2.0, -3.0, -4.0, -6.0])


def pack_weight(w, fmt):
    k, n = w.shape
    w = f64(np.asarray(w, np.float32).astype(ml_dtypes.bfloat16)).reshape(k // 32, 32, n)
    amax = np.abs(w).max(1)
    if fmt == "e4m3":
        byte = np.frexp(amax)[1] - 1 + 127 - 7
    else:
        mant, ex = np.frexp(amax / 6.0)
        byte = np.where(mant > 0.5, ex, ex - 1) + 127
    byte = np.clip(np.where(amax > 0, byte, 1), 1, 254)
    scaled = (w * np.exp2(127.0 - byte)[:, None, :]).reshape(k, n).astype(np.float32)
    by_word = np.ascontiguousarray(scaled.reshape(k // 512, 128, 4, n).transpose(0, 1, 3, 2))
    if fmt == "e4m3":
        words = by_word.astype(ml_dtypes.float8_e4m3fn).view(np.uint8)
    else:
        c = by_word.astype(ml_dtypes.float4_e2m1fn).view(np.uint8) & 0xF
        words = (c[..., 0::2] | (c[..., 1::2] << 4)).reshape(k // 512, 128, 2 * n)
    return np.ascontiguousarray(words), np.ascontiguousarray(byte.astype(np.uint8).reshape(k // 512, 16, n))


def unpack_weight(words, scales, fmt):
    g, _, n = scales.shape
    words = np.ascontiguousarray(words).reshape(g, 128, n, -1)
    if fmt == "e4m3":
        vals = words.view(ml_dtypes.float8_e4m3fn).astype(np.float64)
    else:
        nib = np.empty((g, 128, n, 4), np.uint8)
        nib[..., 0::2] = words & 0xF
        nib[..., 1::2] = words >> 4
        vals = E2M1[nib]
    vals = vals * np.repeat(np.exp2(scales.astype(np.float64) - 127.0), 8, axis=1)[..., None]
    return vals.transpose(0, 1, 3, 2).reshape(g * 512, n)


D, T, U, X, I, Q = 512, 1024, 1024, 1024, 512, 128


def setup_inputs():
    n = np.random.standard_normal
    idx = np.stack([np.random.permutation(T)[:I] for _ in range(8)])
    idx2 = np.stack([np.random.permutation(U)[:I] for _ in range(8)])
    idx3 = np.stack([np.random.permutation(X)[:I] for _ in range(8)])
    idx4 = np.stack([np.random.permutation(X)[:I] for _ in range(8)])
    idx5 = np.stack([np.random.permutation(X)[:I] for _ in range(8)])
    idx6 = np.stack([np.random.permutation(T)[:I] for _ in range(8)])
    fd = mx_kscale(D)
    keysp = pack_weight(n((D, T)) / fd[:, None], "e2m1")
    notesp = pack_weight(n((D, U)) / fd[:, None], "e4m3")
    usersp = pack_weight(n((D, X)) / fd[:, None], "e2m1")
    return {
        "query": (n((D, Q)) * 1.0 / np.sqrt(D) * fd[:, None]).astype(np.float32),
        "keys_words": keysp[0],
        "keys_scales": keysp[1],
        "notes_words": notesp[0],
        "notes_scales": notesp[1],
        "users_words": usersp[0],
        "users_scales": usersp[1],
        "offs": striped8(idx),
        "offs2": striped8(idx2),
        "offs3": striped8(idx3),
        "offs4": striped8(idx4),
        "offs5": striped8(idx5),
        "offs6": striped8(idx6),
    }


def reference(query, keys_words, keys_scales, notes_words, notes_scales, users_words, users_scales, offs, offs2, offs3, offs4, offs5, offs6):
    idx = unstriped8(offs)
    idx2 = unstriped8(offs2)
    idx3 = unstriped8(offs3)
    idx4 = unstriped8(offs4)
    idx5 = unstriped8(offs5)
    idx6 = unstriped8(offs6)
    keysu = unpack_weight(keys_words, keys_scales, "e2m1")
    notesu = unpack_weight(notes_words, notes_scales, "e4m3")
    usersu = unpack_weight(users_words, users_scales, "e2m1")
    queryq = mxq(f64(query), 0, "e4m3")
    a = queryq.T @ keysu
    b = queryq.T @ notesu
    c0 = queryq.T @ usersu
    f1 = np.zeros((Q, X))
    f1[np.arange(Q)[:, None], idx3[np.arange(Q) % 128 // 16]] = pick8(a, idx, 16)
    f2 = np.zeros((Q, X))
    f2[np.arange(Q)[:, None], idx4[np.arange(Q) % 128 // 16]] = pick8(b, idx2, 16)
    m1 = np.maximum(f1, f2)
    cc = c0 - m1
    f3 = np.zeros((Q, T))
    f3[np.arange(Q)[:, None], idx6[np.arange(Q) % 128 // 16]] = pick8(cc, idx5, 16)
    aa = a + f3
    y = pick8(aa, idx, 16)
    return y

@@ -1,0 +1,145 @@
+from contextlib import ExitStack
+
+import concourse.mybir as mybir
+
+D, POOL, SLOTS, Q = 512, 1024, 512, 128
+FLOPS = 3 * 2 * D * Q * POOL
+
+F32 = mybir.dt.float32
+BF16 = mybir.dt.bfloat16
+I32 = mybir.dt.int32
+U32 = mybir.dt.uint32
+U16 = mybir.dt.uint16
+U8 = mybir.dt.uint8
+FP8X4 = mybir.dt.float8_e4m3fn_x4
+FP4X4 = mybir.dt.float4_e2m1fn_x4
+COPY = mybir.ActivationFunctionType.Copy
+ALU = mybir.AluOpType
+
+P = 128
+PACK = 4
+BANK = 512
+HALF = SLOTS // 2
+GROUP = 16
+
+
+def tile_attend_collected_three_kernel(tc, query, keys_words, keys_scales, notes_words, notes_scales,
+                                        users_words, users_scales, offs, offs2, offs3, offs4, offs5, offs6, out):
+    nc = tc.nc
+    with ExitStack() as ctx:
+        sb = ctx.enter_context(tc.tile_pool(name="sb", bufs=1))
+        ps = ctx.enter_context(tc.psum_pool(name="ps", bufs=1))
+
+        def load_list(src, name):
+            t = sb.tile([P, SLOTS // GROUP], U16, name=name)
+            nc.sync.dma_start(t[:], src)
+            return t
+
+        def scale_tile(name):
+            t = sb.tile([P, POOL], U8, name=name, align_bytes=64)
+            nc.vector.memset(t[:].bitcast(U32), 0)
+            return t
+
+        def load_scales(t, src):
+            rows = src[0].bitcast(I32)
+            for quad in range(4):
+                nc.sync.dma_start(t[32 * quad : 32 * quad + 4, :].bitcast(I32), rows[4 * quad : 4 * quad + 4, :])
+
+        def load_words(src2d, width, name):
+            t = sb.tile([P, width], U8, name=name, align_bytes=64)
+            nc.sync.dma_start(t[:].bitcast(I32), src2d.bitcast(I32))
+            return t
+
+        def zeros(name, engine):
+            t = sb.tile([P, POOL], F32, name=name)
+            engine.memset(t[:], 0.0)
+            return t
+
+        def gather_halves(window, offsets, first, second):
+            k = HALF // GROUP
+            nc.vector.tensor_copy(first, window[:].indirect(offsets[:, 0:k]))
+            nc.scalar.activation(second, window[:].indirect(offsets[:, k : 2 * k]), COPY)
+
+        keys_s = scale_tile("keys_s")
+        notes_s = scale_tile("notes_s")
+        users_s = scale_tile("users_s")
+
+        q_raw = sb.tile([P, PACK, Q], F32, name="q_raw")
+        nc.sync.dma_start(q_raw[:], query.rearrange("(p j) q -> p j q", j=PACK))
+        keys_w = load_words(keys_words[0], 2 * POOL, "keys_w")
+        load_scales(keys_s, keys_scales)
+        l1 = load_list(offs, "l1")
+        l3 = load_list(offs3, "l3")
+        notes_w = load_words(notes_words[0].rearrange("p n t -> p (n t)"), 4 * POOL, "notes_w")
+        load_scales(notes_s, notes_scales)
+        l2 = load_list(offs2, "l2")
+        l4 = load_list(offs4, "l4")
+        users_w = load_words(users_words[0], 2 * POOL, "users_w")
+        load_scales(users_s, users_scales)
+        l5 = load_list(offs5, "l5")
+        l6 = load_list(offs6, "l6")
+
+        f1 = zeros("f1", nc.vector)
+        f2 = zeros("f2", nc.vector)
+        f3 = zeros("f3", nc.gpsimd)
+
+        q_bf = sb.tile([P, Q, PACK], BF16, name="q_bf", align_bytes=64)
+        nc.vector.tensor_copy(q_bf[:], q_raw[:].rearrange("p j q -> p q j"))
+        q_w = sb.tile([P, Q], U32, name="q_w", align_bytes=64)
+        q_s = sb.tile([P, Q], U8, name="q_s", align_bytes=64)
+        nc.vector.quantize_mx(out=q_w[:].bitcast(FP8X4), scales=q_s[:], in_=q_bf[:].rearrange("p q j -> p (q j)"))
+
+        def score(words, scales, fmt, word_bytes, c0, n, name):
+            bank = ps.tile([P, n], F32, name=name)
+            nc.tensor.matmul_mx(
+                out=bank[:],
+                lhsT=q_w[:].bitcast(FP8X4),
+                lhsT_scale=q_s[:],
+                rhs=words[:, word_bytes * c0 : word_bytes * (c0 + n)].bitcast(fmt),
+                rhs_scale=scales[:, c0 : c0 + n],
+                start=True,
+                stop=True,
+            )
+            return bank
+
+        a = sb.tile([P, POOL], F32, name="a")
+        quarter = POOL // 4
+        for c in range(4):
+            bank = score(keys_w, keys_s, FP4X4, 2, c * quarter, quarter, "a_ps%d" % c)
+            cols = slice(c * quarter, (c + 1) * quarter)
+            if c % 2 == 0:
+                nc.scalar.activation(a[:, cols], bank[:], COPY)
+            else:
+                nc.vector.tensor_copy(a[:, cols], bank[:])
+        g1 = sb.tile([P, SLOTS], F32, name="g1")
+        gather_halves(a, l1, g1[:, 0:HALF], g1[:, HALF:SLOTS])
+        nc.vector.tensor_copy(f1[:].indirect(l3[:]), g1[:])
+
+        b = sb.tile([P, POOL], F32, name="b")
+        for c in range(2):
+            bank = score(notes_w, notes_s, FP8X4, 4, c * BANK, BANK, "b_ps%d" % c)
+            nc.scalar.activation(b[:, c * BANK : (c + 1) * BANK], bank[:], COPY)
+        g2 = sb.tile([P, SLOTS], F32, name="g2")
+        nc.scalar.activation(g2[:], b[:].indirect(l2[:]), COPY)
+        nc.vector.tensor_copy(f2[:].indirect(l4[:]), g2[:])
+
+        c_ps = [score(users_w, users_s, FP4X4, 2, c * BANK, BANK, "c_ps%d" % c) for c in range(2)]
+        m1 = sb.tile([P, POOL], F32, name="m1")
+        cc = sb.tile([P, POOL], F32, name="cc")
+        for c in range(2):
+            cols = slice(c * BANK, (c + 1) * BANK)
+            nc.vector.tensor_tensor(m1[:, cols], f1[:, cols], f2[:, cols], ALU.max)
+        for c in range(2):
+            cols = slice(c * BANK, (c + 1) * BANK)
+            nc.vector.tensor_tensor(cc[:, cols], c_ps[c][:], m1[:, cols], ALU.subtract)
+        g3 = sb.tile([P, SLOTS], F32, name="g3")
+        gather_halves(cc, l5, g3[:, 0:HALF], g3[:, HALF:SLOTS])
+        nc.vector.tensor_copy(f3[:].indirect(l6[:]), g3[:])
+
+        aa = sb.tile([P, POOL], F32, name="aa")
+        nc.vector.tensor_tensor(aa[:], a[:], f3[:], ALU.add)
+        y0 = sb.tile([P, HALF], F32, name="y0")
+        y1 = sb.tile([P, HALF], F32, name="y1")
+        gather_halves(aa, l1, y0[:], y1[:])
+        nc.sync.dma_start(out[:, 0:HALF], y0[:])
+        nc.scalar.dma_start(out[:, HALF:SLOTS], y1[:])

@@ -50,9 +50,9 @@ def tile_attend_collected_three_kernel(tc, query, keys_words, keys_scales, notes
             nc.sync.dma_start(t[:].bitcast(I32), src2d.bitcast(I32))
             return t
 
-        def zeros(name, engine):
-            t = sb.tile([P, POOL], F32, name=name)
-            engine.memset(t[:], 0.0)
+        def zeros(name, tag):
+            t = sb.tile([P, POOL], F32, name=name, tag=tag, align_bytes=64)
+            nc.vector.memset(t[:], 0.0)
             return t
 
         def gather_halves(window, offsets, first, second):
@@ -68,10 +68,10 @@ def tile_attend_collected_three_kernel(tc, query, keys_words, keys_scales, notes
         nc.sync.dma_start(q_raw[:], query.rearrange("(p j) q -> p j q", j=PACK))
         keys_w = load_words(keys_words[0], 2 * POOL, "keys_w")
         load_scales(keys_s, keys_scales)
-        l1 = load_list(offs, "l1")
-        l3 = load_list(offs3, "l3")
         notes_w = load_words(notes_words[0].rearrange("p n t -> p (n t)"), 4 * POOL, "notes_w")
+        l1 = load_list(offs, "l1")
         load_scales(notes_s, notes_scales)
+        l3 = load_list(offs3, "l3")
         l2 = load_list(offs2, "l2")
         l4 = load_list(offs4, "l4")
         users_w = load_words(users_words[0], 2 * POOL, "users_w")
@@ -79,15 +79,15 @@ def tile_attend_collected_three_kernel(tc, query, keys_words, keys_scales, notes
         l5 = load_list(offs5, "l5")
         l6 = load_list(offs6, "l6")
 
-        f1 = zeros("f1", nc.vector)
-        f2 = zeros("f2", nc.vector)
-        f3 = zeros("f3", nc.gpsimd)
+        f1 = zeros("f1", "f1")
+        f2 = zeros("f2", "f2")
 
-        q_bf = sb.tile([P, Q, PACK], BF16, name="q_bf", align_bytes=64)
+        q_bf = sb.tile([P, Q, PACK], BF16, name="q_bf", tag="q_bf_then_f3", align_bytes=64)
         nc.vector.tensor_copy(q_bf[:], q_raw[:].rearrange("p j q -> p q j"))
         q_w = sb.tile([P, Q], U32, name="q_w", align_bytes=64)
         q_s = sb.tile([P, Q], U8, name="q_s", align_bytes=64)
         nc.vector.quantize_mx(out=q_w[:].bitcast(FP8X4), scales=q_s[:], in_=q_bf[:].rearrange("p q j -> p (q j)"))
+        f3 = zeros("f3", "q_bf_then_f3")
 
         def score(words, scales, fmt, word_bytes, c0, n, name):
             bank = ps.tile([P, n], F32, name=name)
@@ -103,14 +103,14 @@ def tile_attend_collected_three_kernel(tc, query, keys_words, keys_scales, notes
             return bank
 
         a = sb.tile([P, POOL], F32, name="a")
-        quarter = POOL // 4
-        for c in range(4):
-            bank = score(keys_w, keys_s, FP4X4, 2, c * quarter, quarter, "a_ps%d" % c)
-            cols = slice(c * quarter, (c + 1) * quarter)
-            if c % 2 == 0:
-                nc.scalar.activation(a[:, cols], bank[:], COPY)
+        c0 = 0
+        for n, on_scalar in ((512, True), (256, False), (128, False), (128, True)):
+            bank = score(keys_w, keys_s, FP4X4, 2, c0, n, "a_ps%d" % c0)
+            if on_scalar:
+                nc.scalar.activation(a[:, c0 : c0 + n], bank[:], COPY)
             else:
-                nc.vector.tensor_copy(a[:, cols], bank[:])
+                nc.vector.tensor_copy(a[:, c0 : c0 + n], bank[:])
+            c0 = c0 + n
         g1 = sb.tile([P, SLOTS], F32, name="g1")
         gather_halves(a, l1, g1[:, 0:HALF], g1[:, HALF:SLOTS])
         nc.vector.tensor_copy(f1[:].indirect(l3[:]), g1[:])

@@ -21,6 +21,7 @@ PACK = 4
 BANK = 512
 HALF = SLOTS // 2
 GROUP = 16
+SHARE = 320
 
 
 def tile_attend_collected_three_kernel(tc, query, keys_words, keys_scales, notes_words, notes_scales,
@@ -104,8 +105,10 @@ def tile_attend_collected_three_kernel(tc, query, keys_words, keys_scales, notes
 
         a = sb.tile([P, POOL], F32, name="a")
         c0 = 0
+        a_ps = []
         for n, on_scalar in ((512, True), (256, False), (128, False), (128, True)):
             bank = score(keys_w, keys_s, FP4X4, 2, c0, n, "a_ps%d" % c0)
+            a_ps.append(bank)
             if on_scalar:
                 nc.scalar.activation(a[:, c0 : c0 + n], bank[:], COPY)
             else:
@@ -129,15 +132,20 @@ def tile_attend_collected_three_kernel(tc, query, keys_words, keys_scales, notes
         for c in range(2):
             cols = slice(c * BANK, (c + 1) * BANK)
             nc.vector.tensor_tensor(m1[:, cols], f1[:, cols], f2[:, cols], ALU.max)
-        for c in range(2):
-            cols = slice(c * BANK, (c + 1) * BANK)
-            nc.vector.tensor_tensor(cc[:, cols], c_ps[c][:], m1[:, cols], ALU.subtract)
+        c_sb = sb.tile([P, SHARE], F32, name="c_sb")
+        nc.scalar.activation(c_sb[:], c_ps[0][:, 0:SHARE], COPY)
+        nc.gpsimd.tensor_tensor(cc[:, 0:SHARE], c_sb[:], m1[:, 0:SHARE], ALU.subtract)
+        nc.vector.tensor_tensor(cc[:, SHARE:BANK], c_ps[0][:, SHARE:BANK], m1[:, SHARE:BANK], ALU.subtract)
+        nc.vector.tensor_tensor(cc[:, BANK:POOL], c_ps[1][:], m1[:, BANK:POOL], ALU.subtract)
         g3 = sb.tile([P, SLOTS], F32, name="g3")
         gather_halves(cc, l5, g3[:, 0:HALF], g3[:, HALF:SLOTS])
         nc.vector.tensor_copy(f3[:].indirect(l6[:]), g3[:])
 
         aa = sb.tile([P, POOL], F32, name="aa")
-        nc.vector.tensor_tensor(aa[:], a[:], f3[:], ALU.add)
+        cut = POOL - SHARE
+        nc.gpsimd.tensor_tensor(aa[:, cut:POOL], a[:, cut:POOL], f3[:, cut:POOL], ALU.add)
+        nc.vector.tensor_tensor(aa[:, 0:BANK], a_ps[0][:], f3[:, 0:BANK], ALU.add)
+        nc.vector.tensor_tensor(aa[:, BANK:cut], a_ps[1][:, 0 : cut - BANK], f3[:, BANK:cut], ALU.add)
         y0 = sb.tile([P, HALF], F32, name="y0")
         y1 = sb.tile([P, HALF], F32, name="y1")
         gather_halves(aa, l1, y0[:], y1[:])

@@ -21,7 +21,7 @@ PACK = 4
 BANK = 512
 HALF = SLOTS // 2
 GROUP = 16
-SHARE = 320
+SHARE = 256
 
 
 def tile_attend_collected_three_kernel(tc, query, keys_words, keys_scales, notes_words, notes_scales,
@@ -132,11 +132,9 @@ def tile_attend_collected_three_kernel(tc, query, keys_words, keys_scales, notes
         for c in range(2):
             cols = slice(c * BANK, (c + 1) * BANK)
             nc.vector.tensor_tensor(m1[:, cols], f1[:, cols], f2[:, cols], ALU.max)
-        c_sb = sb.tile([P, SHARE], F32, name="c_sb")
-        nc.scalar.activation(c_sb[:], c_ps[0][:, 0:SHARE], COPY)
-        nc.gpsimd.tensor_tensor(cc[:, 0:SHARE], c_sb[:], m1[:, 0:SHARE], ALU.subtract)
-        nc.vector.tensor_tensor(cc[:, SHARE:BANK], c_ps[0][:, SHARE:BANK], m1[:, SHARE:BANK], ALU.subtract)
-        nc.vector.tensor_tensor(cc[:, BANK:POOL], c_ps[1][:], m1[:, BANK:POOL], ALU.subtract)
+        for c in range(2):
+            cols = slice(c * BANK, (c + 1) * BANK)
+            nc.vector.tensor_tensor(cc[:, cols], c_ps[c][:], m1[:, cols], ALU.subtract)
         g3 = sb.tile([P, SLOTS], F32, name="g3")
         gather_halves(cc, l5, g3[:, 0:HALF], g3[:, HALF:SLOTS])
         nc.vector.tensor_copy(f3[:].indirect(l6[:]), g3[:])

from contextlib import ExitStack

import concourse.mybir as mybir

D, POOL, SLOTS, Q = 512, 1024, 512, 128
FLOPS = 3 * 2 * D * Q * POOL

F32 = mybir.dt.float32
BF16 = mybir.dt.bfloat16
I32 = mybir.dt.int32
U32 = mybir.dt.uint32
U16 = mybir.dt.uint16
U8 = mybir.dt.uint8
FP8X4 = mybir.dt.float8_e4m3fn_x4
FP4X4 = mybir.dt.float4_e2m1fn_x4
COPY = mybir.ActivationFunctionType.Copy
ALU = mybir.AluOpType

P = 128
PACK = 4
BANK = 512
HALF = SLOTS // 2
GROUP = 16
SHARE = 256


def tile_attend_collected_three_kernel(tc, query, keys_words, keys_scales, notes_words, notes_scales,
                                        users_words, users_scales, offs, offs2, offs3, offs4, offs5, offs6, out):
    nc = tc.nc
    with ExitStack() as ctx:
        sb = ctx.enter_context(tc.tile_pool(name="sb", bufs=1))
        ps = ctx.enter_context(tc.psum_pool(name="ps", bufs=1))

        def load_list(src, name):
            t = sb.tile([P, SLOTS // GROUP], U16, name=name)
            nc.sync.dma_start(t[:], src)
            return t

        def scale_tile(name):
            t = sb.tile([P, POOL], U8, name=name, align_bytes=64)
            nc.vector.memset(t[:].bitcast(U32), 0)
            return t

        def load_scales(t, src):
            rows = src[0].bitcast(I32)
            for quad in range(4):
                nc.sync.dma_start(t[32 * quad : 32 * quad + 4, :].bitcast(I32), rows[4 * quad : 4 * quad + 4, :])

        def load_words(src2d, width, name):
            t = sb.tile([P, width], U8, name=name, align_bytes=64)
            nc.sync.dma_start(t[:].bitcast(I32), src2d.bitcast(I32))
            return t

        def zeros(name, tag):
            t = sb.tile([P, POOL], F32, name=name, tag=tag, align_bytes=64)
            nc.vector.memset(t[:], 0.0)
            return t

        def gather_halves(window, offsets, first, second):
            k = HALF // GROUP
            nc.vector.tensor_copy(first, window[:].indirect(offsets[:, 0:k]))
            nc.scalar.activation(second, window[:].indirect(offsets[:, k : 2 * k]), COPY)

        keys_s = scale_tile("keys_s")
        notes_s = scale_tile("notes_s")
        users_s = scale_tile("users_s")

        q_raw = sb.tile([P, PACK, Q], F32, name="q_raw")
        nc.sync.dma_start(q_raw[:], query.rearrange("(p j) q -> p j q", j=PACK))
        keys_w = load_words(keys_words[0], 2 * POOL, "keys_w")
        load_scales(keys_s, keys_scales)
        notes_w = load_words(notes_words[0].rearrange("p n t -> p (n t)"), 4 * POOL, "notes_w")
        l1 = load_list(offs, "l1")
        load_scales(notes_s, notes_scales)
        l3 = load_list(offs3, "l3")
        l2 = load_list(offs2, "l2")
        l4 = load_list(offs4, "l4")
        users_w = load_words(users_words[0], 2 * POOL, "users_w")
        load_scales(users_s, users_scales)
        l5 = load_list(offs5, "l5")
        l6 = load_list(offs6, "l6")

        f1 = zeros("f1", "f1")
        f2 = zeros("f2", "f2")

        q_bf = sb.tile([P, Q, PACK], BF16, name="q_bf", tag="q_bf_then_f3", align_bytes=64)
        nc.vector.tensor_copy(q_bf[:], q_raw[:].rearrange("p j q -> p q j"))
        q_w = sb.tile([P, Q], U32, name="q_w", align_bytes=64)
        q_s = sb.tile([P, Q], U8, name="q_s", align_bytes=64)
        nc.vector.quantize_mx(out=q_w[:].bitcast(FP8X4), scales=q_s[:], in_=q_bf[:].rearrange("p q j -> p (q j)"))
        f3 = zeros("f3", "q_bf_then_f3")

        def score(words, scales, fmt, word_bytes, c0, n, name):
            bank = ps.tile([P, n], F32, name=name)
            nc.tensor.matmul_mx(
                out=bank[:],
                lhsT=q_w[:].bitcast(FP8X4),
                lhsT_scale=q_s[:],
                rhs=words[:, word_bytes * c0 : word_bytes * (c0 + n)].bitcast(fmt),
                rhs_scale=scales[:, c0 : c0 + n],
                start=True,
                stop=True,
            )
            return bank

        a = sb.tile([P, POOL], F32, name="a")
        c0 = 0
        a_ps = []
        for n, on_scalar in ((512, True), (256, False), (128, False), (128, True)):
            bank = score(keys_w, keys_s, FP4X4, 2, c0, n, "a_ps%d" % c0)
            a_ps.append(bank)
            if on_scalar:
                nc.scalar.activation(a[:, c0 : c0 + n], bank[:], COPY)
            else:
                nc.vector.tensor_copy(a[:, c0 : c0 + n], bank[:])
            c0 = c0 + n
        g1 = sb.tile([P, SLOTS], F32, name="g1")
        gather_halves(a, l1, g1[:, 0:HALF], g1[:, HALF:SLOTS])
        nc.vector.tensor_copy(f1[:].indirect(l3[:]), g1[:])

        b = sb.tile([P, POOL], F32, name="b")
        for c in range(2):
            bank = score(notes_w, notes_s, FP8X4, 4, c * BANK, BANK, "b_ps%d" % c)
            nc.scalar.activation(b[:, c * BANK : (c + 1) * BANK], bank[:], COPY)
        g2 = sb.tile([P, SLOTS], F32, name="g2")
        nc.scalar.activation(g2[:], b[:].indirect(l2[:]), COPY)
        nc.vector.tensor_copy(f2[:].indirect(l4[:]), g2[:])

        c_ps = [score(users_w, users_s, FP4X4, 2, c * BANK, BANK, "c_ps%d" % c) for c in range(2)]
        m1 = sb.tile([P, POOL], F32, name="m1")
        cc = sb.tile([P, POOL], F32, name="cc")
        for c in range(2):
            cols = slice(c * BANK, (c + 1) * BANK)
            nc.vector.tensor_tensor(m1[:, cols], f1[:, cols], f2[:, cols], ALU.max)
        for c in range(2):
            cols = slice(c * BANK, (c + 1) * BANK)
            nc.vector.tensor_tensor(cc[:, cols], c_ps[c][:], m1[:, cols], ALU.subtract)
        g3 = sb.tile([P, SLOTS], F32, name="g3")
        gather_halves(cc, l5, g3[:, 0:HALF], g3[:, HALF:SLOTS])
        nc.vector.tensor_copy(f3[:].indirect(l6[:]), g3[:])

        aa = sb.tile([P, POOL], F32, name="aa")
        cut = POOL - SHARE
        nc.gpsimd.tensor_tensor(aa[:, cut:POOL], a[:, cut:POOL], f3[:, cut:POOL], ALU.add)
        nc.vector.tensor_tensor(aa[:, 0:BANK], a_ps[0][:], f3[:, 0:BANK], ALU.add)
        nc.vector.tensor_tensor(aa[:, BANK:cut], a_ps[1][:, 0 : cut - BANK], f3[:, BANK:cut], ALU.add)
        y0 = sb.tile([P, HALF], F32, name="y0")
        y1 = sb.tile([P, HALF], F32, name="y1")
        gather_halves(aa, l1, y0[:], y1[:])
        nc.sync.dma_start(out[:, 0:HALF], y0[:])
        nc.scalar.dma_start(out[:, HALF:SLOTS], y1[:])
